import numpy as np
CORES = [83,85,87,115,117,119]
N = 6
F = 64
BOUND = 127
def setup_inputs(rng):
    gr = rng.standard_normal((1, 128, N * F), dtype=np.float32) + rng.standard_normal((N, 128, N * F), dtype=np.float32)
    gr = gr * (2.0 ** rng.uniform(-3, 3, (1, 128, 1))).astype(np.float32)
    return {"gr": gr}
def setup_inputs_big(rng):
    d = setup_inputs(rng)
    for k in ("gr",): d[k] = (d[k].astype(np.float32) * 1024.0).astype(d[k].dtype)
    return d
def setup_inputs_small(rng):
    d = setup_inputs(rng)
    for k in ("gr",): d[k] = (d[k].astype(np.float32) * (1 / 1024.0)).astype(d[k].dtype)
    return d
def setup_inputs_apart(rng):
    d = setup_inputs(rng)
    f = (10.0 ** rng.permutation(np.linspace(-1.5, 1.5, N))).astype(np.float32).reshape(N, 1, 1)
    for k in ("gr",): d[k] = (d[k].astype(np.float32) * f).astype(d[k].dtype)
    return d
def setup_inputs_mixed(rng):
    d = setup_inputs(rng)
    f = (10.0 ** rng.uniform(-3, 3, (1, 128, 1))).astype(np.float32); shape = rng.integers(2, size=(1, 128, 1))
    for k in ("gr",):
        x = d[k].astype(np.float32)
        other = x * np.where(rng.random((1, 128, N * F)) < 0.5, 0.1, 1.0).astype(np.float32)
        d[k] = (np.where(shape == 1, other, x) * f).astype(d[k].dtype)
    return d
def reference(gr):
    s = gr.astype(np.float64).sum(axis=0)
    nrm = np.sqrt((s ** 2).sum(axis=1, keepdims=True))
    s = s * np.minimum(1.0, BOUND / nrm)
    return {"y": np.stack([s[:, F * r:F * r + F] for r in range(N)]).astype(np.float32)}

@@ -1,0 +1,181 @@
+import numpy as np
+from concourse.bass import DstId, RemoteDMATransfer
+from concourse.mybir import AluOpType, AxisListType, ActivationFunctionType
+
+N = 6
+F = 64
+K4 = 57
+DEG = 16
+_CHEB = np.polynomial.chebyshev.chebinterpolate(lambda v: 1.0 / np.sqrt(2.5 + 1.5 * v), DEG)
+COEF = [float(a) for a in np.polynomial.chebyshev.cheb2poly(_CHEB)]
+NQ = 4 + (N - 1)
+
+SCRATCH = {
+    "G": ("sbuf", [128, N * F], "float32"),
+    "land": ("sbuf", [128, (N - 1) * F], "float32"),
+    "acc": ("psum", [128, F], "float32"),
+    "s": ("sbuf", [128, F], "float32"),
+    "junk": ("sbuf", [128, F], "float32"),
+    "qall": ("sbuf", [128, 12], "float32"),
+    "fl": ("sbuf", [128, 12], "float32"),
+    "sc": ("sbuf", [128, 12], "float32"),
+    "four": ("sbuf", [128, K4], "float32"),
+    "thr": ("sbuf", [128, K4], "float32"),
+    "gm": ("sbuf", [128, K4], "float32"),
+    "f": ("sbuf", [128, 1], "float32"),
+    "al": ("sbuf", [128, DEG], "float32"),
+    "xa": ("sbuf", [128, DEG], "float32"),
+    "vt": ("sbuf", [128, DEG], "float32"),
+    "coef": ("sbuf", [128, DEG], "float32"),
+    "hs": ("sbuf", [128, DEG], "float32"),
+    "ysb": ("sbuf", [128, F], "float32"),
+}
+SEMAPHORES = ["ld_off", "ld_on", "arr0", "arr1", "arr2", "arr3", "arr4", "qarr", "snt", "cs", "vs", "ss", "st"]
+
+
+def _bits(m):
+    return [b for b in range(m.bit_length()) if (m >> b) & 1]
+
+
+def _mask(engines):
+    m = 0
+    for b in engines:
+        m |= 1 << b
+    return m
+
+
+def _plan(T, topo, r):
+    cores = T.cores
+    near = [i for i in range(N) if i != r and topo.chip(cores[i]) == topo.chip(cores[r])]
+    far = [i for i in range(N) if topo.chip(cores[i]) != topo.chip(cores[r])]
+    home = sorted(near + [r])
+    last = far[home.index(r) % len(far)]
+    early = [i for i in far if i != last]
+    return near, early, last
+
+
+def _order(T, topo, r):
+    near, early, last = _plan(T, topo, r)
+    return near + early + [last]
+
+
+def rank_program(g, core, T, topo):
+    r = T.rank_of(core)
+    if r is None:
+        return
+    cores = T.cores
+    sem = T.sem
+    V, S, Y = g.vector, g.scalar, g.sync
+    add, mult, mx, sub, gt = AluOpType.add, AluOpType.mult, AluOpType.max, AluOpType.subtract, AluOpType.is_gt
+    bound = float(T.tables["BOUND"])
+    near, early, last = _plan(T, topo, r)
+    far = sorted(early + [last])
+    for i in near + far:
+        assert topo.may_write(core, cores[i])
+
+    def blk(t, j):
+        return t[:, j * F:(j + 1) * F]
+
+    def dst(i):
+        rid, pid, _ = topo.addr(cores[i])
+        return DstId(rid=rid, pnc=pid)
+
+    e_off = _bits(topo.mask(core, cores[far[0]]))
+    e_on = [b for b in _bits(topo.mask(core, cores[near[0]])) if b not in e_off]
+    h_off, h_on = len(e_off) // 2, len(e_on) // 2
+
+    home = sorted(near + [r])
+    c0, c1 = far[0] * F, (far[-1] + 1) * F
+    d0, d1 = home[0] * F, (home[-1] + 1) * F
+    Y.dma_start(T.G[:, c0:c1], T.gr[:, c0:c1]).then_inc(sem.ld_off, 16)
+    Y.dma_start(T.G[:, d0:d1], T.gr[:, d0:d1]).then_inc(sem.ld_on, 16)
+
+    sent = [0]
+
+    def part(i, engines):
+        slot = _order(T, topo, i).index(r)
+        sent[0] += len(engines)
+        return RemoteDMATransfer(dst_ids=[dst(i)], dma_engine_mask=_mask(engines), remote_sem=sem["arr%d" % slot],
+                                 src=blk(T.G, i), dst=blk(T.land, slot))
+
+    g.wait_ge(sem.ld_off, 16)
+    g.remote_dma_fused([part(early[0], e_off[:h_off]), part(early[1], e_off[h_off:])], local_sem=sem.snt)
+    g.wait_ge(sem.ld_on, 16)
+    g.remote_dma_fused([part(near[0], e_on[:h_on]), part(near[1], e_on[h_on:])], local_sem=sem.snt)
+    g.remote_dma_fused([part(last, e_off)], local_sem=sem.snt)
+
+    def column(group, engines):
+        sent[0] += len(engines)
+        cols = [4 + _order(T, topo, i).index(r) for i in group]
+        return RemoteDMATransfer(dst_ids=[dst(i) for i in group], dma_engine_mask=_mask(engines), remote_sem=sem.qarr,
+                                 srcs=[T.qall[:, 0:1]], dsts=[T.qall[:, c:c + 1] for c in cols])
+
+    g.wait_ge(sem.ss, 1)
+    g.remote_dma_fused([column(far, e_off), column(near, e_on)], local_sem=sem.snt)
+    g.wait_ge(sem.snt, sent[0])
+
+    nc = [0]
+
+    def const(inst):
+        inst.then_inc(sem.cs, 1)
+        nc[0] += 1
+
+    const(V.memset(T.four[:], 4.0))
+    const(V.memset(T.fl[:, 0:NQ - 1], 0.0))
+    const(V.memset(T.fl[:, NQ - 1:NQ], 1.0))
+    const(V.memset(T.qall[:, 1:4], 0.0))
+    const(V.memset(T.al[:], 2.0 / 3.0))
+    for t in range(DEG):
+        const(V.memset(T.coef[:, t:t + 1], COEF[DEG - 1 - t]))
+    V.wait_ge(sem.cs, nc[0])
+    const(V.tensor_tensor_scan(T.thr[:], T.four[:], T.four[:], 1.0, mult, mx))
+
+    nv = [0]
+
+    def step(inst):
+        inst.then_inc(sem.vs, 1)
+        nv[0] += 1
+
+    order = _order(T, topo, r)
+    count = {}
+    for i in near:
+        count[i] = h_on
+    for i in early:
+        count[i] = h_off
+    count[last] = len(e_off)
+    V.wait_ge(sem.ld_on, 16)
+    for k, i in enumerate(order):
+        V.wait_ge(sem["arr%d" % k], count[i])
+        if k:
+            V.wait_ge(sem.vs, nv[0])
+        a = blk(T.G, r) if k == 0 else T.acc[:]
+        o = T.s[:] if k == len(order) - 1 else T.acc[:]
+        step(V.tensor_tensor(o, a, blk(T.land, k), add))
+    n_sum = nv[0]
+
+    S.wait_ge(sem.vs, n_sum)
+    S.activation(T.junk[:], T.s[:], ActivationFunctionType.Square, scale=1.0 / bound,
+                 accum_out=T.qall[:, 0:1]).then_inc(sem.ss, 1)
+
+    x = T.sc[:, NQ - 1:NQ]
+    V.wait_ge(sem.cs, nc[0])
+    V.wait_ge(sem.ss, 1)
+    V.wait_ge(sem.qarr, len(far) * len(e_off) + len(near) * len(e_on))
+    V.wait_ge(sem.vs, nv[0])
+    step(V.tensor_tensor_scan(T.sc[:, 0:NQ], T.qall[:, 0:NQ], T.fl[:, 0:NQ], 0.0, add, mx))
+    V.wait_ge(sem.vs, nv[0])
+    step(V.tensor_scalar(T.gm[:], T.thr[:], x, 0.5, gt, mx))
+    V.wait_ge(sem.vs, nv[0])
+    step(V.tensor_reduce(T.f[:], T.gm[:], AxisListType.X, mult))
+    V.wait_ge(sem.vs, nv[0])
+    step(V.tensor_scalar(T.xa[:], T.al[:], x, T.f[:], mult, mult))
+    V.wait_ge(sem.vs, nv[0])
+    step(V.tensor_scalar(T.vt[:], T.xa[:], T.f[:], 5.0 / 3.0, mult, sub))
+    V.wait_ge(sem.vs, nv[0])
+    step(V.tensor_tensor_scan(T.hs[:], T.vt[:], T.coef[:], COEF[DEG], mult, add))
+    V.wait_ge(sem.vs, nv[0])
+    step(V.tensor_scalar(T.ysb[:], T.s[:], T.f[:], T.hs[:, DEG - 1:DEG], mult, mult))
+
+    Y.wait_ge(sem.vs, nv[0])
+    Y.dma_start(T.y[:], T.ysb[:]).then_inc(sem.st, 16)
+    Y.wait_ge(sem.st, 16)

@@ -9,6 +9,8 @@ DEG = 16
 _CHEB = np.polynomial.chebyshev.chebinterpolate(lambda v: 1.0 / np.sqrt(2.5 + 1.5 * v), DEG)
 COEF = [float(a) for a in np.polynomial.chebyshev.cheb2poly(_CHEB)]
 NQ = 4 + (N - 1)
+K2 = 2 * K4
+KS = K2 + DEG
 
 SCRATCH = {
     "G": ("sbuf", [128, N * F], "float32"),
@@ -20,17 +22,16 @@ SCRATCH = {
     "fl": ("sbuf", [128, 12], "float32"),
     "sc": ("sbuf", [128, 12], "float32"),
     "four": ("sbuf", [128, K4], "float32"),
-    "thr": ("sbuf", [128, K4], "float32"),
-    "gm": ("sbuf", [128, K4], "float32"),
+    "thr": ("sbuf", [128, K2], "float32"),
+    "d0": ("sbuf", [128, KS], "float32"),
+    "d1": ("sbuf", [128, KS], "float32"),
+    "so": ("sbuf", [128, KS], "float32"),
     "f": ("sbuf", [128, 1], "float32"),
-    "al": ("sbuf", [128, DEG], "float32"),
-    "xa": ("sbuf", [128, DEG], "float32"),
-    "vt": ("sbuf", [128, DEG], "float32"),
     "coef": ("sbuf", [128, DEG], "float32"),
     "hs": ("sbuf", [128, DEG], "float32"),
     "ysb": ("sbuf", [128, F], "float32"),
 }
-SEMAPHORES = ["ld_off", "ld_on", "arr0", "arr1", "arr2", "arr3", "arr4", "qarr", "snt", "cs", "vs", "ss", "st"]
+SEMAPHORES = ["ld_off", "ld_on", "arr0", "arr1", "arr2", "arr3", "arr4", "qarr", "snt", "cs", "vs", "fs", "ss", "st"]
 
 
 def _bits(m):
@@ -66,7 +67,7 @@ def rank_program(g, core, T, topo):
     cores = T.cores
     sem = T.sem
     V, S, Y = g.vector, g.scalar, g.sync
-    add, mult, mx, sub, gt = AluOpType.add, AluOpType.mult, AluOpType.max, AluOpType.subtract, AluOpType.is_gt
+    add, mult, mx, gt = AluOpType.add, AluOpType.mult, AluOpType.max, AluOpType.is_gt
     bound = float(T.tables["BOUND"])
     near, early, last = _plan(T, topo, r)
     far = sorted(early + [last])
@@ -124,11 +125,16 @@ def rank_program(g, core, T, topo):
     const(V.memset(T.fl[:, 0:NQ - 1], 0.0))
     const(V.memset(T.fl[:, NQ - 1:NQ], 1.0))
     const(V.memset(T.qall[:, 1:4], 0.0))
-    const(V.memset(T.al[:], 2.0 / 3.0))
+    const(V.memset(T.d0[:, K2:K2 + 1], 2.0 / 3.0))
+    const(V.memset(T.d0[:, K2 + 1:KS], 1.0))
+    const(V.memset(T.d1[:, 0:K2], 0.0))
+    const(V.memset(T.d1[:, K2:K2 + 1], -5.0 / 3.0))
+    const(V.memset(T.d1[:, K2 + 1:KS], 0.0))
     for t in range(DEG):
         const(V.memset(T.coef[:, t:t + 1], COEF[DEG - 1 - t]))
     V.wait_ge(sem.cs, nc[0])
-    const(V.tensor_tensor_scan(T.thr[:], T.four[:], T.four[:], 1.0, mult, mx))
+    const(V.tensor_tensor_scan(T.thr[:, 0:K4], T.four[:], T.four[:], 1.0, mult, mx))
+    const(V.tensor_tensor_scan(T.thr[:, K4:K2], T.four[:], T.four[:], 1.0, mult, mx))
 
     nv = [0]
 
@@ -164,15 +170,13 @@ def rank_program(g, core, T, topo):
     V.wait_ge(sem.vs, nv[0])
     step(V.tensor_tensor_scan(T.sc[:, 0:NQ], T.qall[:, 0:NQ], T.fl[:, 0:NQ], 0.0, add, mx))
     V.wait_ge(sem.vs, nv[0])
-    step(V.tensor_scalar(T.gm[:], T.thr[:], x, 0.5, gt, mx))
+    step(V.tensor_scalar(T.d0[:, 0:K2], T.thr[:], x, 0.5, gt, mx))
     V.wait_ge(sem.vs, nv[0])
-    step(V.tensor_reduce(T.f[:], T.gm[:], AxisListType.X, mult))
+    step(V.tensor_tensor_scan(T.so[:], T.d0[:], T.d1[:], x, mult, add))
+    V.tensor_reduce(T.f[:], T.d0[:, 0:K4], AxisListType.X, mult).then_inc(sem.fs, 1)
     V.wait_ge(sem.vs, nv[0])
-    step(V.tensor_scalar(T.xa[:], T.al[:], x, T.f[:], mult, mult))
-    V.wait_ge(sem.vs, nv[0])
-    step(V.tensor_scalar(T.vt[:], T.xa[:], T.f[:], 5.0 / 3.0, mult, sub))
-    V.wait_ge(sem.vs, nv[0])
-    step(V.tensor_tensor_scan(T.hs[:], T.vt[:], T.coef[:], COEF[DEG], mult, add))
+    step(V.tensor_tensor_scan(T.hs[:], T.so[:, K2:KS], T.coef[:], COEF[DEG], mult, add))
+    V.wait_ge(sem.fs, 1)
     V.wait_ge(sem.vs, nv[0])
     step(V.tensor_scalar(T.ysb[:], T.s[:], T.f[:], T.hs[:, DEG - 1:DEG], mult, mult))
 

import numpy as np
from concourse.bass import DstId, RemoteDMATransfer
from concourse.mybir import AluOpType, AxisListType, ActivationFunctionType

N = 6
F = 64
K4 = 57
DEG = 16
_CHEB = np.polynomial.chebyshev.chebinterpolate(lambda v: 1.0 / np.sqrt(2.5 + 1.5 * v), DEG)
COEF = [float(a) for a in np.polynomial.chebyshev.cheb2poly(_CHEB)]
NQ = 4 + (N - 1)
K2 = 2 * K4
KS = K2 + DEG

SCRATCH = {
    "G": ("sbuf", [128, N * F], "float32"),
    "land": ("sbuf", [128, (N - 1) * F], "float32"),
    "acc": ("psum", [128, F], "float32"),
    "s": ("sbuf", [128, F], "float32"),
    "junk": ("sbuf", [128, F], "float32"),
    "qall": ("sbuf", [128, 12], "float32"),
    "fl": ("sbuf", [128, 12], "float32"),
    "sc": ("sbuf", [128, 12], "float32"),
    "four": ("sbuf", [128, K4], "float32"),
    "thr": ("sbuf", [128, K2], "float32"),
    "d0": ("sbuf", [128, KS], "float32"),
    "d1": ("sbuf", [128, KS], "float32"),
    "so": ("sbuf", [128, KS], "float32"),
    "f": ("sbuf", [128, 1], "float32"),
    "coef": ("sbuf", [128, DEG], "float32"),
    "hs": ("sbuf", [128, DEG], "float32"),
    "ysb": ("sbuf", [128, F], "float32"),
}
SEMAPHORES = ["ld_off", "ld_on", "arr0", "arr1", "arr2", "arr3", "arr4", "qarr", "snt", "cs", "vs", "fs", "ss", "st"]


def _bits(m):
    return [b for b in range(m.bit_length()) if (m >> b) & 1]


def _mask(engines):
    m = 0
    for b in engines:
        m |= 1 << b
    return m


def _plan(T, topo, r):
    cores = T.cores
    near = [i for i in range(N) if i != r and topo.chip(cores[i]) == topo.chip(cores[r])]
    far = [i for i in range(N) if topo.chip(cores[i]) != topo.chip(cores[r])]
    home = sorted(near + [r])
    last = far[home.index(r) % len(far)]
    early = [i for i in far if i != last]
    return near, early, last


def _order(T, topo, r):
    near, early, last = _plan(T, topo, r)
    return near + early + [last]


def rank_program(g, core, T, topo):
    r = T.rank_of(core)
    if r is None:
        return
    cores = T.cores
    sem = T.sem
    V, S, Y = g.vector, g.scalar, g.sync
    add, mult, mx, gt = AluOpType.add, AluOpType.mult, AluOpType.max, AluOpType.is_gt
    bound = float(T.tables["BOUND"])
    near, early, last = _plan(T, topo, r)
    far = sorted(early + [last])
    for i in near + far:
        assert topo.may_write(core, cores[i])

    def blk(t, j):
        return t[:, j * F:(j + 1) * F]

    def dst(i):
        rid, pid, _ = topo.addr(cores[i])
        return DstId(rid=rid, pnc=pid)

    e_off = _bits(topo.mask(core, cores[far[0]]))
    e_on = [b for b in _bits(topo.mask(core, cores[near[0]])) if b not in e_off]
    h_off, h_on = len(e_off) // 2, len(e_on) // 2

    home = sorted(near + [r])
    c0, c1 = far[0] * F, (far[-1] + 1) * F
    d0, d1 = home[0] * F, (home[-1] + 1) * F
    Y.dma_start(T.G[:, c0:c1], T.gr[:, c0:c1]).then_inc(sem.ld_off, 16)
    Y.dma_start(T.G[:, d0:d1], T.gr[:, d0:d1]).then_inc(sem.ld_on, 16)

    sent = [0]

    def part(i, engines):
        slot = _order(T, topo, i).index(r)
        sent[0] += len(engines)
        return RemoteDMATransfer(dst_ids=[dst(i)], dma_engine_mask=_mask(engines), remote_sem=sem["arr%d" % slot],
                                 src=blk(T.G, i), dst=blk(T.land, slot))

    g.wait_ge(sem.ld_off, 16)
    g.remote_dma_fused([part(early[0], e_off[:h_off]), part(early[1], e_off[h_off:])], local_sem=sem.snt)
    g.wait_ge(sem.ld_on, 16)
    g.remote_dma_fused([part(near[0], e_on[:h_on]), part(near[1], e_on[h_on:])], local_sem=sem.snt)
    g.remote_dma_fused([part(last, e_off)], local_sem=sem.snt)

    def column(group, engines):
        sent[0] += len(engines)
        cols = [4 + _order(T, topo, i).index(r) for i in group]
        return RemoteDMATransfer(dst_ids=[dst(i) for i in group], dma_engine_mask=_mask(engines), remote_sem=sem.qarr,
                                 srcs=[T.qall[:, 0:1]], dsts=[T.qall[:, c:c + 1] for c in cols])

    g.wait_ge(sem.ss, 1)
    g.remote_dma_fused([column(far, e_off), column(near, e_on)], local_sem=sem.snt)
    g.wait_ge(sem.snt, sent[0])

    nc = [0]

    def const(inst):
        inst.then_inc(sem.cs, 1)
        nc[0] += 1

    const(V.memset(T.four[:], 4.0))
    const(V.memset(T.fl[:, 0:NQ - 1], 0.0))
    const(V.memset(T.fl[:, NQ - 1:NQ], 1.0))
    const(V.memset(T.qall[:, 1:4], 0.0))
    const(V.memset(T.d0[:, K2:K2 + 1], 2.0 / 3.0))
    const(V.memset(T.d0[:, K2 + 1:KS], 1.0))
    const(V.memset(T.d1[:, 0:K2], 0.0))
    const(V.memset(T.d1[:, K2:K2 + 1], -5.0 / 3.0))
    const(V.memset(T.d1[:, K2 + 1:KS], 0.0))
    for t in range(DEG):
        const(V.memset(T.coef[:, t:t + 1], COEF[DEG - 1 - t]))
    V.wait_ge(sem.cs, nc[0])
    const(V.tensor_tensor_scan(T.thr[:, 0:K4], T.four[:], T.four[:], 1.0, mult, mx))
    const(V.tensor_tensor_scan(T.thr[:, K4:K2], T.four[:], T.four[:], 1.0, mult, mx))

    nv = [0]

    def step(inst):
        inst.then_inc(sem.vs, 1)
        nv[0] += 1

    order = _order(T, topo, r)
    count = {}
    for i in near:
        count[i] = h_on
    for i in early:
        count[i] = h_off
    count[last] = len(e_off)
    V.wait_ge(sem.ld_on, 16)
    for k, i in enumerate(order):
        V.wait_ge(sem["arr%d" % k], count[i])
        if k:
            V.wait_ge(sem.vs, nv[0])
        a = blk(T.G, r) if k == 0 else T.acc[:]
        o = T.s[:] if k == len(order) - 1 else T.acc[:]
        step(V.tensor_tensor(o, a, blk(T.land, k), add))
    n_sum = nv[0]

    S.wait_ge(sem.vs, n_sum)
    S.activation(T.junk[:], T.s[:], ActivationFunctionType.Square, scale=1.0 / bound,
                 accum_out=T.qall[:, 0:1]).then_inc(sem.ss, 1)

    x = T.sc[:, NQ - 1:NQ]
    V.wait_ge(sem.cs, nc[0])
    V.wait_ge(sem.ss, 1)
    V.wait_ge(sem.qarr, len(far) * len(e_off) + len(near) * len(e_on))
    V.wait_ge(sem.vs, nv[0])
    step(V.tensor_tensor_scan(T.sc[:, 0:NQ], T.qall[:, 0:NQ], T.fl[:, 0:NQ], 0.0, add, mx))
    V.wait_ge(sem.vs, nv[0])
    step(V.tensor_scalar(T.d0[:, 0:K2], T.thr[:], x, 0.5, gt, mx))
    V.wait_ge(sem.vs, nv[0])
    step(V.tensor_tensor_scan(T.so[:], T.d0[:], T.d1[:], x, mult, add))
    V.tensor_reduce(T.f[:], T.d0[:, 0:K4], AxisListType.X, mult).then_inc(sem.fs, 1)
    V.wait_ge(sem.vs, nv[0])
    step(V.tensor_tensor_scan(T.hs[:], T.so[:, K2:KS], T.coef[:], COEF[DEG], mult, add))
    V.wait_ge(sem.fs, 1)
    V.wait_ge(sem.vs, nv[0])
    step(V.tensor_scalar(T.ysb[:], T.s[:], T.f[:], T.hs[:, DEG - 1:DEG], mult, mult))

    Y.wait_ge(sem.vs, nv[0])
    Y.dma_start(T.y[:], T.ysb[:]).then_inc(sem.st, 16)
    Y.wait_ge(sem.st, 16)
